import numpy as np
import ml_dtypes


def mxq(x, axis, fmt="e4m3"):
    dtype, down = {"e4m3": (ml_dtypes.float8_e4m3fn, 7), "e5m2": (ml_dtypes.float8_e5m2, 14)}[fmt]
    v = np.moveaxis(np.asarray(x, np.float32).astype(ml_dtypes.bfloat16).astype(np.float64), axis, -1)
    blocks = v.reshape(v.shape[:-1] + (-1, 32))
    amax = np.abs(blocks).max(-1, keepdims=True)
    byte = np.maximum(np.where(amax > 0, np.frexp(amax)[1] - 1 + 127, 0) - down, 1)
    scale = np.exp2(byte - 127.0)
    codes = (blocks / scale).astype(np.float32).astype(dtype).astype(np.float64)
    return np.moveaxis((codes * scale).reshape(v.shape), -1, axis)


WIDE = False


def mx_kscale(k):
    if not WIDE:
        return np.ones(k)
    levels = np.array([10, -10, 5, -5, 0])
    if k % 512:
        return np.exp2(np.random.permutation(np.resize(levels, k // 32))).repeat(32)
    a = np.empty((k // 512, 16))
    for p in range(k // 512):
        a[p, :8] = np.random.permutation(np.resize(levels, 8))
        for g in range(8):
            far = levels[np.abs(levels - a[p, g]) >= 10]
            a[p, g + 8] = far[np.random.randint(len(far))]
    return np.exp2(a.ravel()).repeat(32)


def f64(x):
    return np.asarray(x).astype(np.float64)


def striped(idx):
    return np.tile(idx.reshape(-1, 16).T, (8, 1)).astype(np.uint16)


def unstriped(offs):
    return offs[:16].T.reshape(-1).astype(np.int64)


K, T, E, C, N = 1024, 2048, 8, 256, 128


def by_expert(wq, xq):
    return np.concatenate([wq[e].T @ xq[:, e * C:(e + 1) * C] for e in range(E)], axis=1)


def setup_inputs():
    n = np.random.standard_normal
    s = mx_kscale(K)[:, None]
    return {
        "xT": (n((K, T)) * s).astype(np.float32),
        "w": (n((E, K, N)) / np.sqrt(K) / s[None]).astype(np.float32),
        "b": (0.3 * n((N, E))).astype(np.float32),
        "gate": np.tile(np.random.uniform(0.2, 1.0, E * C), (N, 1)).astype(np.float32),
        "offs": striped(np.random.permutation(T)[:E * C]),
    }


def reference(xT, w, b, gate, offs):
    idx = unstriped(offs)
    xq = mxq(f64(xT)[:, idx], 0, "e4m3")
    y = by_expert(mxq(f64(w), 1, "e4m3"), xq)
    y = y + np.repeat(f64(b), C, axis=1)
    out = np.zeros((N, T))
    out[:, idx] = f64(gate) * y
    return out

@@ -1,0 +1,184 @@
+from contextlib import ExitStack
+
+import concourse.mybir as mybir
+
+K, T, E, C, N = 1024, 2048, 8, 256, 128
+FLOPS = 2 * K * E * C * N
+
+F32 = mybir.dt.float32
+BF16 = mybir.dt.bfloat16
+U32 = mybir.dt.uint32
+U16 = mybir.dt.uint16
+U8 = mybir.dt.uint8
+FP8X4 = mybir.dt.float8_e4m3fn_x4
+MULT = mybir.AluOpType.mult
+IDENT = mybir.ActivationFunctionType.Identity
+
+P = 128
+PACK = 4
+PASSES = K // (P * PACK)
+CHUNK = 512
+CHUNKS = E * C // CHUNK
+OCOLS = CHUNK // 16
+PER = CHUNK // C
+
+
+def tile_routed_moe_kernel(tc, xT, w, b, gate, offs, out):
+    nc = tc.nc
+    with ExitStack() as ctx:
+        keep = ctx.enter_context(tc.tile_pool(name="keep", bufs=1))
+        ring = ctx.enter_context(tc.tile_pool(name="ring", bufs=1))
+        psum = ctx.enter_context(tc.psum_pool(name="psum", bufs=1))
+
+        offsets = keep.tile([P, E * C // 16], U16, name="offsets")
+        nc.sync.dma_start(offsets[:], offs)
+
+        x_planes = xT.rearrange("(g p t) n -> g p t n", p=P, t=PACK)
+        w_rows = w.rearrange("e (g p j) n -> p (e g) (j n)", g=PASSES, p=P, j=PACK)
+        planes = {}
+        w_raw = {}
+
+        def load_plane(g, t):
+            plane = keep.tile([P, T], F32, name="plane%d%d" % (g, t))
+            nc.sync.dma_start(plane[:], x_planes[g, :, t, :])
+            planes[(g, t)] = plane
+
+        def load_w(q):
+            raw = keep.tile([P, 4, PACK * N], F32, name="w_raw%d" % q)
+            nc.sync.dma_start(raw[:], w_rows[:, 4 * q : 4 * q + 4, :])
+            w_raw[q] = raw
+
+        load_plane(0, 0)
+        load_plane(0, 1)
+        load_w(0)
+        load_w(1)
+        load_plane(0, 2)
+        load_plane(0, 3)
+        load_w(2)
+        load_w(3)
+        for t in range(PACK):
+            load_plane(1, t)
+        gate_sb = keep.tile([P, E * C], F32, name="gate_sb")
+        nc.sync.dma_start(gate_sb[:], gate)
+        b_sb = keep.tile([P, E], F32, name="b_sb")
+        nc.sync.dma_start(b_sb[:], b)
+
+        window = keep.tile([P, T], F32, name="window")
+
+        w_codes = {}
+        w_scales = {}
+        w_grouped = {}
+
+        def interleave_w(q):
+            grouped = ring.tile([P, 4, N, PACK], BF16, name="w_grouped", bufs=2, align_bytes=64)
+            nc.scalar.copy(
+                out=grouped[:],
+                in_=w_raw[q][:].rearrange("p a (j n) -> p a n j", j=PACK),
+            )
+            w_grouped[q] = grouped
+
+        def quantize_w(q):
+            codes = keep.tile([P, 4 * N], U32, name="w_codes%d" % q, align_bytes=64)
+            scales = keep.tile([P, 4 * N], U8, name="w_scales%d" % q, align_bytes=64)
+            nc.vector.quantize_mx(
+                out=codes[:].bitcast(FP8X4),
+                scales=scales[:],
+                in_=w_grouped[q][:].rearrange("p a n j -> p (a n j)"),
+            )
+            w_codes[q] = codes
+            w_scales[q] = scales
+
+        picked = {}
+        x_grouped = {}
+        x_codes = {}
+        x_scales = {}
+        sums = {}
+
+        def gather(g, t, c):
+            if t == 0:
+                picked[(g, c)] = ring.tile([P, PACK, CHUNK], F32, name="picked", bufs=6)
+            nc.vector.tensor_copy(
+                picked[(g, c)][:, t, :],
+                planes[(g, t)][:].indirect(offsets[:, OCOLS * c : OCOLS * (c + 1)]),
+            )
+
+        def interleave_x(g, c):
+            grouped = ring.tile([P, CHUNK, PACK], BF16, name="x_grouped", bufs=3, align_bytes=64)
+            nc.scalar.copy(out=grouped[:], in_=picked[(g, c)][:].rearrange("p t n -> p n t"))
+            x_grouped[(g, c)] = grouped
+
+        def quantize_x(g, c):
+            codes = keep.tile([P, CHUNK], U32, name="x_codes%d%d" % (g, c), align_bytes=64)
+            scales = keep.tile([P, CHUNK], U8, name="x_scales%d%d" % (g, c), align_bytes=64)
+            nc.vector.quantize_mx(
+                out=codes[:].bitcast(FP8X4),
+                scales=scales[:],
+                in_=x_grouped[(g, c)][:].rearrange("p n t -> p (n t)"),
+            )
+            x_codes[(g, c)] = codes
+            x_scales[(g, c)] = scales
+
+        def multiply(c):
+            y = keep.tile([P, CHUNK], F32, name="y%d" % c)
+            for h in range(PER):
+                e = PER * c + h
+                acc = psum.tile([P, C], F32, name="acc%d" % e)
+                slots = slice(C * h, C * (h + 1))
+                for g in range(PASSES):
+                    cols = slice(N * (PASSES * h + g), N * (PASSES * h + g + 1))
+                    nc.tensor.matmul_mx(
+                        out=acc[:],
+                        lhsT=w_codes[c][:, cols].bitcast(FP8X4),
+                        lhsT_scale=w_scales[c][:, cols],
+                        rhs=x_codes[(g, c)][:, slots].bitcast(FP8X4),
+                        rhs_scale=x_scales[(g, c)][:, slots],
+                        start=(g == 0),
+                        stop=(g == PASSES - 1),
+                    )
+                nc.scalar.activation(out=y[:, slots], in_=acc[:], func=IDENT, bias=b_sb[:, e : e + 1])
+            sums[c] = y
+
+        def scatter(c):
+            nc.vector.tensor_tensor(
+                window[:].indirect(offsets[:, OCOLS * c : OCOLS * (c + 1)]),
+                sums[c][:],
+                gate_sb[:, CHUNK * c : CHUNK * (c + 1)],
+                MULT,
+            )
+
+        for q in range(4):
+            interleave_w(q)
+
+        for t in range(PACK - 1):
+            for c in range(CHUNKS):
+                gather(0, t, c)
+            if t == 1:
+                quantize_w(0)
+                quantize_w(1)
+            if t == 2:
+                quantize_w(2)
+                quantize_w(3)
+        for c in range(CHUNKS):
+            gather(0, PACK - 1, c)
+            interleave_x(0, c)
+            if c >= 1:
+                quantize_x(0, c - 1)
+        for t in range(PACK - 1):
+            for c in range(CHUNKS):
+                gather(1, t, c)
+            if t == 0:
+                quantize_x(0, CHUNKS - 1)
+        for c in range(CHUNKS):
+            gather(1, PACK - 1, c)
+            interleave_x(1, c)
+            if c >= 1:
+                quantize_x(1, c - 1)
+                multiply(c - 1)
+            if c >= 2:
+                scatter(c - 2)
+        quantize_x(1, CHUNKS - 1)
+        multiply(CHUNKS - 1)
+        scatter(CHUNKS - 2)
+        scatter(CHUNKS - 1)
+
+        nc.sync.dma_start(out, window[:])

@@ -12,7 +12,7 @@ U16 = mybir.dt.uint16
 U8 = mybir.dt.uint8
 FP8X4 = mybir.dt.float8_e4m3fn_x4
 MULT = mybir.AluOpType.mult
-IDENT = mybir.ActivationFunctionType.Identity
+ADD = mybir.AluOpType.add
 
 P = 128
 PACK = 4
@@ -35,18 +35,16 @@ def tile_routed_moe_kernel(tc, xT, w, b, gate, offs, out):
 
         x_planes = xT.rearrange("(g p t) n -> g p t n", p=P, t=PACK)
         w_rows = w.rearrange("e (g p j) n -> p (e g) (j n)", g=PASSES, p=P, j=PACK)
-        planes = {}
+        raw = [keep.tile([P, PACK, T], F32, name="raw%d" % g) for g in range(PASSES)]
         w_raw = {}
 
         def load_plane(g, t):
-            plane = keep.tile([P, T], F32, name="plane%d%d" % (g, t))
-            nc.sync.dma_start(plane[:], x_planes[g, :, t, :])
-            planes[(g, t)] = plane
+            nc.sync.dma_start(raw[g][:, t, :], x_planes[g, :, t, :])
 
         def load_w(q):
-            raw = keep.tile([P, 4, PACK * N], F32, name="w_raw%d" % q)
-            nc.sync.dma_start(raw[:], w_rows[:, 4 * q : 4 * q + 4, :])
-            w_raw[q] = raw
+            wr = keep.tile([P, 4, PACK * N], F32, name="w_raw%d" % q)
+            nc.sync.dma_start(wr[:], w_rows[:, 4 * q : 4 * q + 4, :])
+            w_raw[q] = wr
 
         load_plane(0, 0)
         load_plane(0, 1)
@@ -88,7 +86,6 @@ def tile_routed_moe_kernel(tc, xT, w, b, gate, offs, out):
             w_codes[q] = codes
             w_scales[q] = scales
 
-        picked = {}
         x_grouped = {}
         x_codes = {}
         x_scales = {}
@@ -96,16 +93,11 @@ def tile_routed_moe_kernel(tc, xT, w, b, gate, offs, out):
 
         def gather(g, t, c):
             if t == 0:
-                picked[(g, c)] = ring.tile([P, PACK, CHUNK], F32, name="picked", bufs=6)
+                x_grouped[(g, c)] = keep.tile([P, CHUNK, PACK], BF16, name="x_grouped%d%d" % (g, c), align_bytes=64)
             nc.vector.tensor_copy(
-                picked[(g, c)][:, t, :],
-                planes[(g, t)][:].indirect(offsets[:, OCOLS * c : OCOLS * (c + 1)]),
+                x_grouped[(g, c)][:, :, t],
+                raw[g][:, t, :].indirect(offsets[:, OCOLS * c : OCOLS * (c + 1)]),
             )
-
-        def interleave_x(g, c):
-            grouped = ring.tile([P, CHUNK, PACK], BF16, name="x_grouped", bufs=3, align_bytes=64)
-            nc.scalar.copy(out=grouped[:], in_=picked[(g, c)][:].rearrange("p t n -> p n t"))
-            x_grouped[(g, c)] = grouped
 
         def quantize_x(g, c):
             codes = keep.tile([P, CHUNK], U32, name="x_codes%d%d" % (g, c), align_bytes=64)
@@ -118,11 +110,13 @@ def tile_routed_moe_kernel(tc, xT, w, b, gate, offs, out):
             x_codes[(g, c)] = codes
             x_scales[(g, c)] = scales
 
+        accs = {}
+
         def multiply(c):
-            y = keep.tile([P, CHUNK], F32, name="y%d" % c)
             for h in range(PER):
                 e = PER * c + h
                 acc = psum.tile([P, C], F32, name="acc%d" % e)
+                accs[e] = acc
                 slots = slice(C * h, C * (h + 1))
                 for g in range(PASSES):
                     cols = slice(N * (PASSES * h + g), N * (PASSES * h + g + 1))
@@ -135,50 +129,55 @@ def tile_routed_moe_kernel(tc, xT, w, b, gate, offs, out):
                         start=(g == 0),
                         stop=(g == PASSES - 1),
                     )
-                nc.scalar.activation(out=y[:, slots], in_=acc[:], func=IDENT, bias=b_sb[:, e : e + 1])
+
+        def finish(c):
+            y = keep.tile([P, CHUNK], F32, name="y%d" % c)
+            for h in range(PER):
+                e = PER * c + h
+                nc.vector.scalar_tensor_tensor(
+                    out=y[:, C * h : C * (h + 1)],
+                    in0=accs[e][:],
+                    scalar=b_sb[:, e : e + 1],
+                    in1=gate_sb[:, C * e : C * (e + 1)],
+                    op0=ADD,
+                    op1=MULT,
+                )
             sums[c] = y
 
         def scatter(c):
-            nc.vector.tensor_tensor(
+            nc.vector.tensor_copy(
                 window[:].indirect(offsets[:, OCOLS * c : OCOLS * (c + 1)]),
                 sums[c][:],
-                gate_sb[:, CHUNK * c : CHUNK * (c + 1)],
-                MULT,
             )
 
         for q in range(4):
             interleave_w(q)
 
-        for t in range(PACK - 1):
+        for t in range(PACK):
             for c in range(CHUNKS):
                 gather(0, t, c)
+                if t == PACK - 1 and c >= 1:
+                    quantize_x(0, c - 1)
             if t == 1:
                 quantize_w(0)
                 quantize_w(1)
             if t == 2:
                 quantize_w(2)
                 quantize_w(3)
-        for c in range(CHUNKS):
-            gather(0, PACK - 1, c)
-            interleave_x(0, c)
-            if c >= 1:
-                quantize_x(0, c - 1)
         for t in range(PACK - 1):
             for c in range(CHUNKS):
                 gather(1, t, c)
-            if t == 0:
-                quantize_x(0, CHUNKS - 1)
-        for c in range(CHUNKS):
-            gather(1, PACK - 1, c)
-            interleave_x(1, c)
-            if c >= 1:
+                if t == 0 and c == 0:
+                    quantize_x(0, CHUNKS - 1)
+        for c in range(CHUNKS + 3):
+            if c < CHUNKS:
+                gather(1, PACK - 1, c)
+            if 1 <= c <= CHUNKS:
                 quantize_x(1, c - 1)
                 multiply(c - 1)
-            if c >= 2:
-                scatter(c - 2)
-        quantize_x(1, CHUNKS - 1)
-        multiply(CHUNKS - 1)
-        scatter(CHUNKS - 2)
-        scatter(CHUNKS - 1)
+            if 2 <= c <= CHUNKS + 1:
+                finish(c - 2)
+            if c >= 3:
+                scatter(c - 3)
 
         nc.sync.dma_start(out, window[:])

@@ -13,6 +13,7 @@ U8 = mybir.dt.uint8
 FP8X4 = mybir.dt.float8_e4m3fn_x4
 MULT = mybir.AluOpType.mult
 ADD = mybir.AluOpType.add
+COPY = mybir.ActivationFunctionType.Copy
 
 P = 128
 PACK = 4
@@ -21,6 +22,10 @@ CHUNK = 512
 CHUNKS = E * C // CHUNK
 OCOLS = CHUNK // 16
 PER = CHUNK // C
+V_CHUNKS = (0, 1)
+S_CHUNKS = (2, 3)
+S_WEIGHTS = (0, 1)
+BIG = 9
 
 
 def tile_routed_moe_kernel(tc, xT, w, b, gate, offs, out):
@@ -35,44 +40,43 @@ def tile_routed_moe_kernel(tc, xT, w, b, gate, offs, out):
 
         x_planes = xT.rearrange("(g p t) n -> g p t n", p=P, t=PACK)
         w_rows = w.rearrange("e (g p j) n -> p (e g) (j n)", g=PASSES, p=P, j=PACK)
-        raw = [keep.tile([P, PACK, T], F32, name="raw%d" % g) for g in range(PASSES)]
+        planes = {}
         w_raw = {}
-
-        def load_plane(g, t):
-            nc.sync.dma_start(raw[g][:, t, :], x_planes[g, :, t, :])
-
-        def load_w(q):
-            wr = keep.tile([P, 4, PACK * N], F32, name="w_raw%d" % q)
+        for g in range(PASSES):
+            for t in range(PACK):
+                plane = ring.tile([P, T], F32, name="big", bufs=BIG)
+                nc.sync.dma_start(plane[:], x_planes[g, :, t, :])
+                planes[(g, t)] = plane
+        for q in range(CHUNKS):
+            wr = ring.tile([P, 4, PACK * N], F32, name="big", bufs=BIG)
             nc.sync.dma_start(wr[:], w_rows[:, 4 * q : 4 * q + 4, :])
             w_raw[q] = wr
-
-        load_plane(0, 0)
-        load_plane(0, 1)
-        load_w(0)
-        load_w(1)
-        load_plane(0, 2)
-        load_plane(0, 3)
-        load_w(2)
-        load_w(3)
-        for t in range(PACK):
-            load_plane(1, t)
-        gate_sb = keep.tile([P, E * C], F32, name="gate_sb")
+        gate_sb = ring.tile([P, E * C], F32, name="big", bufs=BIG)
         nc.sync.dma_start(gate_sb[:], gate)
         b_sb = keep.tile([P, E], F32, name="b_sb")
         nc.sync.dma_start(b_sb[:], b)
+        window = ring.tile([P, T], F32, name="big", bufs=BIG)
 
-        window = keep.tile([P, T], F32, name="window")
+        rounded = [keep.tile([P, PACK, T], BF16, name="rounded%d" % g) for g in range(PASSES)]
+
+        def round_plane(g, t):
+            for s in range(2):
+                cols = slice(s * T // 2, (s + 1) * T // 2)
+                nc.gpsimd.tensor_scalar(
+                    out=rounded[g][:, t, cols], in0=planes[(g, t)][:, cols], scalar1=1.0, scalar2=0.0, op0=MULT, op1=ADD
+                )
 
         w_codes = {}
         w_scales = {}
         w_grouped = {}
 
         def interleave_w(q):
-            grouped = ring.tile([P, 4, N, PACK], BF16, name="w_grouped", bufs=2, align_bytes=64)
-            nc.scalar.copy(
-                out=grouped[:],
-                in_=w_raw[q][:].rearrange("p a (j n) -> p a n j", j=PACK),
-            )
+            grouped = ring.tile([P, 4, N, PACK], BF16, name="w_grouped", bufs=4, align_bytes=64)
+            src = w_raw[q][:].rearrange("p a (j n) -> p a n j", j=PACK)
+            if q in S_WEIGHTS:
+                nc.scalar.copy(out=grouped[:], in_=src)
+            else:
+                nc.vector.tensor_copy(out=grouped[:], in_=src)
             w_grouped[q] = grouped
 
         def quantize_w(q):
@@ -86,18 +90,30 @@ def tile_routed_moe_kernel(tc, xT, w, b, gate, offs, out):
             w_codes[q] = codes
             w_scales[q] = scales
 
+        picked = {}
         x_grouped = {}
         x_codes = {}
         x_scales = {}
+        accs = {}
         sums = {}
 
-        def gather(g, t, c):
+        def list_of(c):
+            return offsets[:, OCOLS * c : OCOLS * (c + 1)]
+
+        def gather_v(g, t, c):
+            if t == 0:
+                picked[(g, c)] = keep.tile([P, PACK, CHUNK], F32, name="picked%d%d" % (g, c))
+            nc.vector.tensor_copy(picked[(g, c)][:, t, :], planes[(g, t)][:].indirect(list_of(c)))
+
+        def interleave_x(g, c):
+            grouped = keep.tile([P, CHUNK, PACK], BF16, name="x_grouped%d%d" % (g, c), align_bytes=64)
+            nc.vector.tensor_copy(out=grouped[:], in_=picked[(g, c)][:].rearrange("p t n -> p n t"))
+            x_grouped[(g, c)] = grouped
+
+        def gather_s(g, t, c):
             if t == 0:
                 x_grouped[(g, c)] = keep.tile([P, CHUNK, PACK], BF16, name="x_grouped%d%d" % (g, c), align_bytes=64)
-            nc.vector.tensor_copy(
-                x_grouped[(g, c)][:, :, t],
-                raw[g][:, t, :].indirect(offsets[:, OCOLS * c : OCOLS * (c + 1)]),
-            )
+            nc.scalar.activation(x_grouped[(g, c)][:, :, t], rounded[g][:, t, :].indirect(list_of(c)), COPY)
 
         def quantize_x(g, c):
             codes = keep.tile([P, CHUNK], U32, name="x_codes%d%d" % (g, c), align_bytes=64)
@@ -109,8 +125,6 @@ def tile_routed_moe_kernel(tc, xT, w, b, gate, offs, out):
             )
             x_codes[(g, c)] = codes
             x_scales[(g, c)] = scales
-
-        accs = {}
 
         def multiply(c):
             for h in range(PER):
@@ -145,39 +159,48 @@ def tile_routed_moe_kernel(tc, xT, w, b, gate, offs, out):
             sums[c] = y
 
         def scatter(c):
-            nc.vector.tensor_copy(
-                window[:].indirect(offsets[:, OCOLS * c : OCOLS * (c + 1)]),
-                sums[c][:],
-            )
+            nc.vector.tensor_copy(window[:].indirect(list_of(c)), sums[c][:])
 
-        for q in range(4):
-            interleave_w(q)
+        for g in range(PASSES):
+            for t in range(PACK):
+                round_plane(g, t)
+                for c in V_CHUNKS:
+                    gather_v(g, t, c)
+                for c in S_CHUNKS:
+                    gather_s(g, t, c)
+                if (g, t) == (1, 1):
+                    for q in S_WEIGHTS:
+                        interleave_w(q)
 
-        for t in range(PACK):
-            for c in range(CHUNKS):
-                gather(0, t, c)
-                if t == PACK - 1 and c >= 1:
-                    quantize_x(0, c - 1)
-            if t == 1:
-                quantize_w(0)
-                quantize_w(1)
-            if t == 2:
-                quantize_w(2)
-                quantize_w(3)
-        for t in range(PACK - 1):
-            for c in range(CHUNKS):
-                gather(1, t, c)
-                if t == 0 and c == 0:
-                    quantize_x(0, CHUNKS - 1)
-        for c in range(CHUNKS + 3):
-            if c < CHUNKS:
-                gather(1, PACK - 1, c)
-            if 1 <= c <= CHUNKS:
-                quantize_x(1, c - 1)
-                multiply(c - 1)
-            if 2 <= c <= CHUNKS + 1:
-                finish(c - 2)
-            if c >= 3:
-                scatter(c - 3)
+        interleave_x(0, 0)
+        interleave_x(0, 1)
+        quantize_x(0, 0)
+        interleave_x(1, 0)
+        quantize_x(0, 1)
+        interleave_x(1, 1)
+        quantize_x(1, 0)
+        quantize_x(0, 2)
+        quantize_x(1, 1)
+        quantize_x(0, 3)
+        interleave_w(2)
+        quantize_w(0)
+        interleave_w(3)
+        quantize_w(1)
+        multiply(0)
+        multiply(1)
+        quantize_w(2)
+        quantize_w(3)
+        finish(0)
+        scatter(0)
+        finish(1)
+        scatter(1)
+        quantize_x(1, 2)
+        multiply(2)
+        quantize_x(1, 3)
+        multiply(3)
+        finish(2)
+        scatter(2)
+        finish(3)
+        scatter(3)
 
         nc.sync.dma_start(out, window[:])

@@ -18,13 +18,10 @@ COPY = mybir.ActivationFunctionType.Copy
 P = 128
 PACK = 4
 PASSES = K // (P * PACK)
-CHUNK = 512
-CHUNKS = E * C // CHUNK
-OCOLS = CHUNK // 16
-PER = CHUNK // C
-V_CHUNKS = (0, 1)
-S_CHUNKS = (2, 3)
-S_WEIGHTS = (0, 1)
+V_SLOTS = 1024
+S_SLOTS = E * C - V_SLOTS
+PIECE = 512
+V_ROUNDS = ((1, 2), (1, 3))
 BIG = 9
 
 
@@ -47,7 +44,7 @@ def tile_routed_moe_kernel(tc, xT, w, b, gate, offs, out):
                 plane = ring.tile([P, T], F32, name="big", bufs=BIG)
                 nc.sync.dma_start(plane[:], x_planes[g, :, t, :])
                 planes[(g, t)] = plane
-        for q in range(CHUNKS):
+        for q in range(4):
             wr = ring.tile([P, 4, PACK * N], F32, name="big", bufs=BIG)
             nc.sync.dma_start(wr[:], w_rows[:, 4 * q : 4 * q + 4, :])
             w_raw[q] = wr
@@ -57,26 +54,23 @@ def tile_routed_moe_kernel(tc, xT, w, b, gate, offs, out):
         nc.sync.dma_start(b_sb[:], b)
         window = ring.tile([P, T], F32, name="big", bufs=BIG)
 
-        rounded = [keep.tile([P, PACK, T], BF16, name="rounded%d" % g) for g in range(PASSES)]
+        halves = [keep.tile([P, 2, T], BF16, name="rounded%d" % i) for i in range(2 * PASSES)]
 
-        def round_plane(g, t):
-            for s in range(2):
-                cols = slice(s * T // 2, (s + 1) * T // 2)
-                nc.gpsimd.tensor_scalar(
-                    out=rounded[g][:, t, cols], in0=planes[(g, t)][:, cols], scalar1=1.0, scalar2=0.0, op0=MULT, op1=ADD
-                )
+        def rounded(g, t):
+            return halves[2 * g + t // 2][:, t % 2, :]
+
+        picked = [keep.tile([P, PACK, V_SLOTS], F32, name="picked%d" % g) for g in range(PASSES)]
+
+        def list_of(first, n):
+            return offsets[:, first // 16 : (first + n) // 16]
 
         w_codes = {}
         w_scales = {}
         w_grouped = {}
 
         def interleave_w(q):
-            grouped = ring.tile([P, 4, N, PACK], BF16, name="w_grouped", bufs=4, align_bytes=64)
-            src = w_raw[q][:].rearrange("p a (j n) -> p a n j", j=PACK)
-            if q in S_WEIGHTS:
-                nc.scalar.copy(out=grouped[:], in_=src)
-            else:
-                nc.vector.tensor_copy(out=grouped[:], in_=src)
+            grouped = keep.tile([P, 4, N, PACK], BF16, name="w_grouped%d" % q, tag="w_grouped%d" % q, align_bytes=64)
+            nc.vector.tensor_copy(out=grouped[:], in_=w_raw[q][:].rearrange("p a (j n) -> p a n j", j=PACK))
             w_grouped[q] = grouped
 
         def quantize_w(q):
@@ -87,67 +81,50 @@ def tile_routed_moe_kernel(tc, xT, w, b, gate, offs, out):
                 scales=scales[:],
                 in_=w_grouped[q][:].rearrange("p a n j -> p (a n j)"),
             )
-            w_codes[q] = codes
-            w_scales[q] = scales
+            for a in range(4):
+                w_codes[(2 * q + a // 2, a % 2)] = codes[:, N * a : N * (a + 1)]
+                w_scales[(2 * q + a // 2, a % 2)] = scales[:, N * a : N * (a + 1)]
 
-        picked = {}
         x_grouped = {}
         x_codes = {}
         x_scales = {}
         accs = {}
         sums = {}
 
-        def list_of(c):
-            return offsets[:, OCOLS * c : OCOLS * (c + 1)]
+        def grouped_tile(g, first, n):
+            x_grouped[(g, first)] = keep.tile([P, n, PACK], BF16, name="x_grouped%d_%d" % (g, first), align_bytes=64)
 
-        def gather_v(g, t, c):
-            if t == 0:
-                picked[(g, c)] = keep.tile([P, PACK, CHUNK], F32, name="picked%d%d" % (g, c))
-            nc.vector.tensor_copy(picked[(g, c)][:, t, :], planes[(g, t)][:].indirect(list_of(c)))
-
-        def interleave_x(g, c):
-            grouped = keep.tile([P, CHUNK, PACK], BF16, name="x_grouped%d%d" % (g, c), align_bytes=64)
-            nc.vector.tensor_copy(out=grouped[:], in_=picked[(g, c)][:].rearrange("p t n -> p n t"))
-            x_grouped[(g, c)] = grouped
-
-        def gather_s(g, t, c):
-            if t == 0:
-                x_grouped[(g, c)] = keep.tile([P, CHUNK, PACK], BF16, name="x_grouped%d%d" % (g, c), align_bytes=64)
-            nc.scalar.activation(x_grouped[(g, c)][:, :, t], rounded[g][:, t, :].indirect(list_of(c)), COPY)
-
-        def quantize_x(g, c):
-            codes = keep.tile([P, CHUNK], U32, name="x_codes%d%d" % (g, c), align_bytes=64)
-            scales = keep.tile([P, CHUNK], U8, name="x_scales%d%d" % (g, c), align_bytes=64)
+        def quantize_x(g, first, after=None):
+            grouped = x_grouped[(g, first)]
+            n = grouped.shape[1]
+            name = "x_codes%d_%d" % (g, first)
+            codes = keep.tile([P, n], U32, name=name, tag=(after or name), align_bytes=64)
+            scales = keep.tile([P, n], U8, name="x_scales%d_%d" % (g, first), align_bytes=64)
             nc.vector.quantize_mx(
-                out=codes[:].bitcast(FP8X4),
-                scales=scales[:],
-                in_=x_grouped[(g, c)][:].rearrange("p n t -> p (n t)"),
+                out=codes[:].bitcast(FP8X4), scales=scales[:], in_=grouped[:].rearrange("p n t -> p (n t)")
             )
-            x_codes[(g, c)] = codes
-            x_scales[(g, c)] = scales
+            for h in range(n // C):
+                x_codes[(first // C + h, g)] = codes[:, C * h : C * (h + 1)]
+                x_scales[(first // C + h, g)] = scales[:, C * h : C * (h + 1)]
 
-        def multiply(c):
-            for h in range(PER):
-                e = PER * c + h
-                acc = psum.tile([P, C], F32, name="acc%d" % e)
-                accs[e] = acc
-                slots = slice(C * h, C * (h + 1))
-                for g in range(PASSES):
-                    cols = slice(N * (PASSES * h + g), N * (PASSES * h + g + 1))
-                    nc.tensor.matmul_mx(
-                        out=acc[:],
-                        lhsT=w_codes[c][:, cols].bitcast(FP8X4),
-                        lhsT_scale=w_scales[c][:, cols],
-                        rhs=x_codes[(g, c)][:, slots].bitcast(FP8X4),
-                        rhs_scale=x_scales[(g, c)][:, slots],
-                        start=(g == 0),
-                        stop=(g == PASSES - 1),
-                    )
+        def multiply(e):
+            acc = psum.tile([P, C], F32, name="acc%d" % e)
+            accs[e] = acc
+            for g in range(PASSES):
+                nc.tensor.matmul_mx(
+                    out=acc[:],
+                    lhsT=w_codes[(e, g)].bitcast(FP8X4),
+                    lhsT_scale=w_scales[(e, g)],
+                    rhs=x_codes[(e, g)].bitcast(FP8X4),
+                    rhs_scale=x_scales[(e, g)],
+                    start=(g == 0),
+                    stop=(g == PASSES - 1),
+                )
 
-        def finish(c):
-            y = keep.tile([P, CHUNK], F32, name="y%d" % c)
-            for h in range(PER):
-                e = PER * c + h
+        def finish(first):
+            y = keep.tile([P, PIECE], F32, name="y%d" % first, tag="y%d" % first, align_bytes=64)
+            for h in range(PIECE // C):
+                e = first // C + h
                 nc.vector.scalar_tensor_tensor(
                     out=y[:, C * h : C * (h + 1)],
                     in0=accs[e][:],
@@ -156,51 +133,58 @@ def tile_routed_moe_kernel(tc, xT, w, b, gate, offs, out):
                     op0=ADD,
                     op1=MULT,
                 )
-            sums[c] = y
+            sums[first] = y
 
-        def scatter(c):
-            nc.vector.tensor_copy(window[:].indirect(list_of(c)), sums[c][:])
+        def scatter(first):
+            nc.vector.tensor_copy(window[:].indirect(list_of(first, PIECE)), sums[first][:])
+
+        def gather_s(g, t):
+            if g == 0:
+                pieces = ((V_SLOTS, S_SLOTS),)
+            else:
+                pieces = tuple((first, PIECE) for first in range(V_SLOTS, E * C, PIECE))
+            for first, n in pieces:
+                if t == 0:
+                    grouped_tile(g, first, n)
+                nc.scalar.activation(x_grouped[(g, first)][:, :, t], rounded(g, t).indirect(list_of(first, n)), COPY)
 
         for g in range(PASSES):
             for t in range(PACK):
-                round_plane(g, t)
-                for c in V_CHUNKS:
-                    gather_v(g, t, c)
-                for c in S_CHUNKS:
-                    gather_s(g, t, c)
-                if (g, t) == (1, 1):
-                    for q in S_WEIGHTS:
-                        interleave_w(q)
+                nc.vector.tensor_copy(picked[g][:, t, :], planes[(g, t)][:].indirect(list_of(0, V_SLOTS)))
+                if (g, t) not in V_ROUNDS:
+                    nc.scalar.copy(out=rounded(g, t), in_=planes[(g, t)][:])
+                    gather_s(g, t)
+        for g, t in V_ROUNDS:
+            nc.vector.tensor_copy(out=rounded(g, t), in_=planes[(g, t)][:])
+        for g, t in V_ROUNDS:
+            gather_s(g, t)
 
-        interleave_x(0, 0)
-        interleave_x(0, 1)
+        for g in range(PASSES):
+            grouped_tile(g, 0, V_SLOTS)
+            nc.vector.tensor_copy(out=x_grouped[(g, 0)][:], in_=picked[g][:].rearrange("p t n -> p n t"))
+        interleave_w(0)
         quantize_x(0, 0)
-        interleave_x(1, 0)
-        quantize_x(0, 1)
-        interleave_x(1, 1)
+        interleave_w(1)
         quantize_x(1, 0)
-        quantize_x(0, 2)
-        quantize_x(1, 1)
-        quantize_x(0, 3)
-        interleave_w(2)
         quantize_w(0)
-        interleave_w(3)
+        interleave_w(2)
         quantize_w(1)
-        multiply(0)
-        multiply(1)
+        for e in range(4):
+            multiply(e)
+        interleave_w(3)
         quantize_w(2)
+        quantize_x(0, V_SLOTS, after="w_grouped1")
         quantize_w(3)
         finish(0)
+        finish(PIECE)
         scatter(0)
-        finish(1)
-        scatter(1)
-        quantize_x(1, 2)
-        multiply(2)
-        quantize_x(1, 3)
-        multiply(3)
-        finish(2)
-        scatter(2)
-        finish(3)
-        scatter(3)
+        scatter(PIECE)
+        for first in range(V_SLOTS, E * C, PIECE):
+            quantize_x(1, first, after="y%d" % (first - V_SLOTS))
+            for h in range(PIECE // C):
+                multiply(first // C + h)
+        for first in range(V_SLOTS, E * C, PIECE):
+            finish(first)
+            scatter(first)
 
         nc.sync.dma_start(out, window[:])

@@ -18,10 +18,11 @@ COPY = mybir.ActivationFunctionType.Copy
 P = 128
 PACK = 4
 PASSES = K // (P * PACK)
-V_SLOTS = 1024
+V_SLOTS = 512
 S_SLOTS = E * C - V_SLOTS
-PIECE = 512
-V_ROUNDS = ((1, 2), (1, 3))
+S_PIECES = tuple((first, 256) for first in range(512, 2048, 256))
+S_QUANT0 = ((512, 1024), (1536, 512))
+S_ROUNDS = ()
 BIG = 9
 
 
@@ -85,45 +86,42 @@ def tile_routed_moe_kernel(tc, xT, w, b, gate, offs, out):
                 w_codes[(2 * q + a // 2, a % 2)] = codes[:, N * a : N * (a + 1)]
                 w_scales[(2 * q + a // 2, a % 2)] = scales[:, N * a : N * (a + 1)]
 
-        x_grouped = {}
         x_codes = {}
         x_scales = {}
         accs = {}
         sums = {}
 
         def grouped_tile(g, first, n):
-            x_grouped[(g, first)] = keep.tile([P, n, PACK], BF16, name="x_grouped%d_%d" % (g, first), align_bytes=64)
+            name = "x_grouped%d_%d" % (g, first)
+            return keep.tile([P, n, PACK], BF16, name=name, tag=name, align_bytes=64)
 
-        def quantize_x(g, first, after=None):
-            grouped = x_grouped[(g, first)]
-            n = grouped.shape[1]
+        def quantize_x(g, first, n, values, after=None):
             name = "x_codes%d_%d" % (g, first)
             codes = keep.tile([P, n], U32, name=name, tag=(after or name), align_bytes=64)
             scales = keep.tile([P, n], U8, name="x_scales%d_%d" % (g, first), align_bytes=64)
-            nc.vector.quantize_mx(
-                out=codes[:].bitcast(FP8X4), scales=scales[:], in_=grouped[:].rearrange("p n t -> p (n t)")
-            )
+            nc.vector.quantize_mx(out=codes[:].bitcast(FP8X4), scales=scales[:], in_=values.rearrange("p n t -> p (n t)"))
             for h in range(n // C):
                 x_codes[(first // C + h, g)] = codes[:, C * h : C * (h + 1)]
                 x_scales[(first // C + h, g)] = scales[:, C * h : C * (h + 1)]
 
-        def multiply(e):
-            acc = psum.tile([P, C], F32, name="acc%d" % e)
-            accs[e] = acc
-            for g in range(PASSES):
-                nc.tensor.matmul_mx(
-                    out=acc[:],
-                    lhsT=w_codes[(e, g)].bitcast(FP8X4),
-                    lhsT_scale=w_scales[(e, g)],
-                    rhs=x_codes[(e, g)].bitcast(FP8X4),
-                    rhs_scale=x_scales[(e, g)],
-                    start=(g == 0),
-                    stop=(g == PASSES - 1),
-                )
+        def multiply(first, n):
+            for e in range(first // C, (first + n) // C):
+                acc = psum.tile([P, C], F32, name="acc%d" % e)
+                accs[e] = acc
+                for g in range(PASSES):
+                    nc.tensor.matmul_mx(
+                        out=acc[:],
+                        lhsT=w_codes[(e, g)].bitcast(FP8X4),
+                        lhsT_scale=w_scales[(e, g)],
+                        rhs=x_codes[(e, g)].bitcast(FP8X4),
+                        rhs_scale=x_scales[(e, g)],
+                        start=(g == 0),
+                        stop=(g == PASSES - 1),
+                    )
 
-        def finish(first):
-            y = keep.tile([P, PIECE], F32, name="y%d" % first, tag="y%d" % first, align_bytes=64)
-            for h in range(PIECE // C):
+        def finish(first, n):
+            y = keep.tile([P, n], F32, name="y%d" % first, tag="y%d" % first, align_bytes=64)
+            for h in range(n // C):
                 e = first // C + h
                 nc.vector.scalar_tensor_tensor(
                     out=y[:, C * h : C * (h + 1)],
@@ -135,56 +133,56 @@ def tile_routed_moe_kernel(tc, xT, w, b, gate, offs, out):
                 )
             sums[first] = y
 
-        def scatter(first):
-            nc.vector.tensor_copy(window[:].indirect(list_of(first, PIECE)), sums[first][:])
+        def scatter(first, n):
+            nc.vector.tensor_copy(window[:].indirect(list_of(first, n)), sums[first][:])
 
-        def gather_s(g, t):
-            if g == 0:
-                pieces = ((V_SLOTS, S_SLOTS),)
-            else:
-                pieces = tuple((first, PIECE) for first in range(V_SLOTS, E * C, PIECE))
-            for first, n in pieces:
-                if t == 0:
-                    grouped_tile(g, first, n)
-                nc.scalar.activation(x_grouped[(g, first)][:, :, t], rounded(g, t).indirect(list_of(first, n)), COPY)
-
+        s_grouped0 = grouped_tile(0, V_SLOTS, S_SLOTS)
         for g in range(PASSES):
             for t in range(PACK):
-                nc.vector.tensor_copy(picked[g][:, t, :], planes[(g, t)][:].indirect(list_of(0, V_SLOTS)))
-                if (g, t) not in V_ROUNDS:
+                if (g, t) in S_ROUNDS:
                     nc.scalar.copy(out=rounded(g, t), in_=planes[(g, t)][:])
-                    gather_s(g, t)
-        for g, t in V_ROUNDS:
-            nc.vector.tensor_copy(out=rounded(g, t), in_=planes[(g, t)][:])
-        for g, t in V_ROUNDS:
-            gather_s(g, t)
+                else:
+                    nc.vector.tensor_copy(out=rounded(g, t), in_=planes[(g, t)][:])
+                nc.vector.tensor_copy(picked[g][:, t, :], planes[(g, t)][:].indirect(list_of(0, V_SLOTS)))
+                if g == 0:
+                    nc.scalar.activation(s_grouped0[:, :, t], rounded(g, t).indirect(list_of(V_SLOTS, S_SLOTS)), COPY)
+        s_grouped1 = {}
+        last = None
+        for first, n in S_PIECES:
+            s_grouped1[first] = grouped_tile(1, first, n)
+            if last is not None:
+                nc.scalar.copy(out=s_grouped1[first][:, 0, 0:3], in_=last)
+            last = s_grouped1[first][:, n - 3 : n, 3]
+            for t in (3, 0, 1, 2):
+                nc.scalar.activation(s_grouped1[first][:, :, t], rounded(1, t).indirect(list_of(first, n)), COPY)
 
+        v_grouped = []
         for g in range(PASSES):
-            grouped_tile(g, 0, V_SLOTS)
-            nc.vector.tensor_copy(out=x_grouped[(g, 0)][:], in_=picked[g][:].rearrange("p t n -> p n t"))
+            v_grouped.append(grouped_tile(g, 0, V_SLOTS))
+            nc.vector.tensor_copy(out=v_grouped[g][:], in_=picked[g][:].rearrange("p t n -> p n t"))
         interleave_w(0)
-        quantize_x(0, 0)
+        quantize_x(0, 0, V_SLOTS, v_grouped[0][:])
         interleave_w(1)
-        quantize_x(1, 0)
+        quantize_x(1, 0, V_SLOTS, v_grouped[1][:])
         quantize_w(0)
+        multiply(0, V_SLOTS)
         interleave_w(2)
         quantize_w(1)
-        for e in range(4):
-            multiply(e)
         interleave_w(3)
         quantize_w(2)
-        quantize_x(0, V_SLOTS, after="w_grouped1")
         quantize_w(3)
-        finish(0)
-        finish(PIECE)
-        scatter(0)
-        scatter(PIECE)
-        for first in range(V_SLOTS, E * C, PIECE):
-            quantize_x(1, first, after="y%d" % (first - V_SLOTS))
-            for h in range(PIECE // C):
-                multiply(first // C + h)
-        for first in range(V_SLOTS, E * C, PIECE):
-            finish(first)
-            scatter(first)
+        for i, (first, n) in enumerate(S_QUANT0):
+            lo = first - V_SLOTS
+            quantize_x(0, first, n, s_grouped0[:, lo : lo + n, :], after="w_grouped%d" % (2 + i))
+
+        done = [(0, V_SLOTS)] + list(S_PIECES)
+        hold = ["x_grouped0_%d" % V_SLOTS] + ["y%d" % first for first, n in done]
+        for i, (first, n) in enumerate(done):
+            finish(first, n)
+            if i + 1 < len(done):
+                nxt, m = done[i + 1]
+                quantize_x(1, nxt, m, s_grouped1[nxt][:], after=hold[i])
+                multiply(nxt, m)
+            scatter(first, n)
 
         nc.sync.dma_start(out, window[:])

@@ -14,175 +14,237 @@ FP8X4 = mybir.dt.float8_e4m3fn_x4
 MULT = mybir.AluOpType.mult
 ADD = mybir.AluOpType.add
 COPY = mybir.ActivationFunctionType.Copy
+IDENTITY = mybir.ActivationFunctionType.Identity
 
 P = 128
 PACK = 4
 PASSES = K // (P * PACK)
-V_SLOTS = 512
-S_SLOTS = E * C - V_SLOTS
-S_PIECES = tuple((first, 256) for first in range(512, 2048, 256))
-S_QUANT0 = ((512, 1024), (1536, 512))
+V0 = 512
+S0 = ((512, 1024), (1536, 512))
+PIECES = ((0, 512), (512, 512), (1024, 512), (1536, 512))
 S_ROUNDS = ()
-BIG = 9
+S_FINISH = (4, 5, 6, 7)
 
 
 def tile_routed_moe_kernel(tc, xT, w, b, gate, offs, out):
     nc = tc.nc
     with ExitStack() as ctx:
         keep = ctx.enter_context(tc.tile_pool(name="keep", bufs=1))
-        ring = ctx.enter_context(tc.tile_pool(name="ring", bufs=1))
         psum = ctx.enter_context(tc.psum_pool(name="psum", bufs=1))
+
+        def sb(shape, dtype, name, tag=None):
+            return keep.tile(shape, dtype, name=name, tag=(tag or name), align_bytes=64)
 
         offsets = keep.tile([P, E * C // 16], U16, name="offsets")
         nc.sync.dma_start(offsets[:], offs)
+        b_sb = sb([P, E], F32, "b_sb")
 
         x_planes = xT.rearrange("(g p t) n -> g p t n", p=P, t=PACK)
         w_rows = w.rearrange("e (g p j) n -> p (e g) (j n)", g=PASSES, p=P, j=PACK)
         planes = {}
-        w_raw = {}
         for g in range(PASSES):
             for t in range(PACK):
-                plane = ring.tile([P, T], F32, name="big", bufs=BIG)
-                nc.sync.dma_start(plane[:], x_planes[g, :, t, :])
-                planes[(g, t)] = plane
-        for q in range(4):
-            wr = ring.tile([P, 4, PACK * N], F32, name="big", bufs=BIG)
-            nc.sync.dma_start(wr[:], w_rows[:, 4 * q : 4 * q + 4, :])
-            w_raw[q] = wr
-        gate_sb = ring.tile([P, E * C], F32, name="big", bufs=BIG)
-        nc.sync.dma_start(gate_sb[:], gate)
-        b_sb = keep.tile([P, E], F32, name="b_sb")
+                planes[(g, t)] = sb([P, T], F32, "plane%d" % (PACK * g + t))
+                if (g, t) == (0, 0):
+                    for h in range(2):
+                        half = slice(h * T // 2, (h + 1) * T // 2)
+                        nc.sync.dma_start(planes[(g, t)][:, half], x_planes[g, :, t, half])
+                else:
+                    nc.sync.dma_start(planes[(g, t)][:], x_planes[g, :, t, :])
         nc.sync.dma_start(b_sb[:], b)
-        window = ring.tile([P, T], F32, name="big", bufs=BIG)
+        w_raw = {}
+        for q in range(4):
+            w_raw[q] = sb([P, 4, PACK * N], F32, "w_raw%d" % q, "plane%d" % q)
+            nc.sync.dma_start(w_raw[q][:], w_rows[:, 4 * q : 4 * q + 4, :])
+        gate_sb = sb([P, E * C], F32, "gate_sb", "plane4")
+        nc.sync.dma_start(gate_sb[:], gate)
+        window = sb([P, T], F32, "window", "plane6")
 
-        halves = [keep.tile([P, 2, T], BF16, name="rounded%d" % i) for i in range(2 * PASSES)]
+        halves = [sb([P, 2, T], BF16, "rounded%d" % i) for i in range(2 * PASSES)]
 
         def rounded(g, t):
             return halves[2 * g + t // 2][:, t % 2, :]
 
-        picked = [keep.tile([P, PACK, V_SLOTS], F32, name="picked%d" % g) for g in range(PASSES)]
-
         def list_of(first, n):
             return offsets[:, first // 16 : (first + n) // 16]
+
+        def round_plane(g, t):
+            if (g, t) == (0, 0):
+                for h in range(2):
+                    half = slice(h * T // 2, (h + 1) * T // 2)
+                    nc.vector.tensor_copy(out=rounded(g, t)[:, half], in_=planes[(g, t)][:, half])
+            elif (g, t) in S_ROUNDS:
+                nc.scalar.copy(out=rounded(g, t), in_=planes[(g, t)][:])
+            else:
+                nc.vector.tensor_copy(out=rounded(g, t), in_=planes[(g, t)][:])
+
+        def s_gather(pairs, lo, g, t, first, n):
+            nc.scalar.activation(pairs[:, t // 2, lo : lo + n, t % 2], rounded(g, t).indirect(list_of(first, n)), COPY)
+
+        def order_copy(dst_pairs, src_pairs, n, t):
+            nc.scalar.copy(
+                out=dst_pairs[:, :, 0, :],
+                in_=src_pairs[:, t // 2, n - 4 : n, t % 2].rearrange("p (a b) -> p a b", a=2),
+            )
+
+        def join_pairs(name, n, pairs, after):
+            values = sb([P, n, PACK], BF16, name, after)
+            nc.vector.tensor_copy(
+                out=values[:].rearrange("p n (u e) -> p n u e", u=2), in_=pairs.rearrange("p u n e -> p n u e")
+            )
+            return values
+
+        x_codes = {}
+        x_scales = {}
+
+        def quantize_x(g, first, n, values):
+            codes = sb([P, n], U32, "x_codes%d_%d" % (g, first))
+            scales = sb([P, n], U8, "x_scales%d_%d" % (g, first))
+            nc.vector.quantize_mx(out=codes[:].bitcast(FP8X4), scales=scales[:], in_=values.rearrange("p n t -> p (n t)"))
+            for h in range(n // C):
+                x_codes[(first // C + h, g)] = codes[:, C * h : C * (h + 1)]
+                x_scales[(first // C + h, g)] = scales[:, C * h : C * (h + 1)]
 
         w_codes = {}
         w_scales = {}
         w_grouped = {}
 
         def interleave_w(q):
-            grouped = keep.tile([P, 4, N, PACK], BF16, name="w_grouped%d" % q, tag="w_grouped%d" % q, align_bytes=64)
-            nc.vector.tensor_copy(out=grouped[:], in_=w_raw[q][:].rearrange("p a (j n) -> p a n j", j=PACK))
-            w_grouped[q] = grouped
+            w_grouped[q] = sb([P, 4, N, PACK], BF16, "w_grouped%d" % q)
+            nc.vector.tensor_copy(out=w_grouped[q][:], in_=w_raw[q][:].rearrange("p a (j n) -> p a n j", j=PACK))
 
         def quantize_w(q):
-            codes = keep.tile([P, 4 * N], U32, name="w_codes%d" % q, align_bytes=64)
-            scales = keep.tile([P, 4 * N], U8, name="w_scales%d" % q, align_bytes=64)
+            codes = sb([P, 4 * N], U32, "w_codes%d" % q)
+            scales = sb([P, 4 * N], U8, "w_scales%d" % q)
             nc.vector.quantize_mx(
-                out=codes[:].bitcast(FP8X4),
-                scales=scales[:],
-                in_=w_grouped[q][:].rearrange("p a n j -> p (a n j)"),
+                out=codes[:].bitcast(FP8X4), scales=scales[:], in_=w_grouped[q][:].rearrange("p a n j -> p (a n j)")
             )
             for a in range(4):
                 w_codes[(2 * q + a // 2, a % 2)] = codes[:, N * a : N * (a + 1)]
                 w_scales[(2 * q + a // 2, a % 2)] = scales[:, N * a : N * (a + 1)]
 
-        x_codes = {}
-        x_scales = {}
         accs = {}
+
+        def multiply(e, g):
+            if g == 0:
+                accs[e] = psum.tile([P, C], F32, name="acc%d" % e)
+            nc.tensor.matmul_mx(
+                out=accs[e][:],
+                lhsT=w_codes[(e, g)].bitcast(FP8X4),
+                lhsT_scale=w_scales[(e, g)],
+                rhs=x_codes[(e, g)].bitcast(FP8X4),
+                rhs_scale=x_scales[(e, g)],
+                start=(g == 0),
+                stop=(g == PASSES - 1),
+            )
+
         sums = {}
 
-        def grouped_tile(g, first, n):
-            name = "x_grouped%d_%d" % (g, first)
-            return keep.tile([P, n, PACK], BF16, name=name, tag=name, align_bytes=64)
+        def y_tag(i):
+            if i == 2:
+                return "rounded3"
+            if i == 3:
+                return "rounded2"
+            return "y%d" % i
 
-        def quantize_x(g, first, n, values, after=None):
-            name = "x_codes%d_%d" % (g, first)
-            codes = keep.tile([P, n], U32, name=name, tag=(after or name), align_bytes=64)
-            scales = keep.tile([P, n], U8, name="x_scales%d_%d" % (g, first), align_bytes=64)
-            nc.vector.quantize_mx(out=codes[:].bitcast(FP8X4), scales=scales[:], in_=values.rearrange("p n t -> p (n t)"))
-            for h in range(n // C):
-                x_codes[(first // C + h, g)] = codes[:, C * h : C * (h + 1)]
-                x_scales[(first // C + h, g)] = scales[:, C * h : C * (h + 1)]
-
-        def multiply(first, n):
-            for e in range(first // C, (first + n) // C):
-                acc = psum.tile([P, C], F32, name="acc%d" % e)
-                accs[e] = acc
-                for g in range(PASSES):
-                    nc.tensor.matmul_mx(
-                        out=acc[:],
-                        lhsT=w_codes[(e, g)].bitcast(FP8X4),
-                        lhsT_scale=w_scales[(e, g)],
-                        rhs=x_codes[(e, g)].bitcast(FP8X4),
-                        rhs_scale=x_scales[(e, g)],
-                        start=(g == 0),
-                        stop=(g == PASSES - 1),
-                    )
-
-        def finish(first, n):
-            y = keep.tile([P, n], F32, name="y%d" % first, tag="y%d" % first, align_bytes=64)
-            for h in range(n // C):
-                e = first // C + h
+        def finish(i, e):
+            first, n = PIECES[i]
+            if i not in sums:
+                sums[i] = sb([P, n], F32, "y%d" % i, y_tag(i))
+            y = sums[i][:, C * e - first : C * (e + 1) - first]
+            if e in S_FINISH:
+                nc.scalar.activation(out=y, in_=accs[e][:], func=IDENTITY, bias=b_sb[:, e : e + 1])
+            else:
                 nc.vector.scalar_tensor_tensor(
-                    out=y[:, C * h : C * (h + 1)],
+                    out=y,
                     in0=accs[e][:],
                     scalar=b_sb[:, e : e + 1],
                     in1=gate_sb[:, C * e : C * (e + 1)],
                     op0=ADD,
                     op1=MULT,
                 )
-            sums[first] = y
 
-        def scatter(first, n):
-            nc.vector.tensor_copy(window[:].indirect(list_of(first, n)), sums[first][:])
+        def scatter(i):
+            lo, n = PIECES[i]
+            if lo // C in S_FINISH:
+                nc.vector.tensor_tensor(window[:].indirect(list_of(lo, n)), sums[i][:], gate_sb[:, lo : lo + n], MULT)
+            else:
+                nc.vector.tensor_copy(window[:].indirect(list_of(lo, n)), sums[i][:])
 
-        s_grouped0 = grouped_tile(0, V_SLOTS, S_SLOTS)
-        for g in range(PASSES):
-            for t in range(PACK):
-                if (g, t) in S_ROUNDS:
-                    nc.scalar.copy(out=rounded(g, t), in_=planes[(g, t)][:])
-                else:
-                    nc.vector.tensor_copy(out=rounded(g, t), in_=planes[(g, t)][:])
-                nc.vector.tensor_copy(picked[g][:, t, :], planes[(g, t)][:].indirect(list_of(0, V_SLOTS)))
-                if g == 0:
-                    nc.scalar.activation(s_grouped0[:, :, t], rounded(g, t).indirect(list_of(V_SLOTS, S_SLOTS)), COPY)
-        s_grouped1 = {}
-        last = None
-        for first, n in S_PIECES:
-            s_grouped1[first] = grouped_tile(1, first, n)
-            if last is not None:
-                nc.scalar.copy(out=s_grouped1[first][:, 0, 0:3], in_=last)
-            last = s_grouped1[first][:, n - 3 : n, 3]
-            for t in (3, 0, 1, 2):
-                nc.scalar.activation(s_grouped1[first][:, :, t], rounded(1, t).indirect(list_of(first, n)), COPY)
+        pairs_v0 = sb([P, 2, V0, 2], BF16, "pairs_v0")
+        pairs0 = [sb([P, 2, n, 2], BF16, "pairs0_%d" % first) for first, n in S0]
+        pairs1 = [sb([P, 2, n, 2], BF16, "pairs1_%d" % first) for first, n in PIECES]
+        for t in range(PACK):
+            round_plane(0, t)
+            nc.vector.tensor_copy(pairs_v0[:, t // 2, :, t % 2], planes[(0, t)][:].indirect(list_of(0, V0)))
+            s_gather(pairs0[0], 0, 0, t, S0[0][0], S0[0][1])
+        order_copy(pairs0[1], pairs0[0], S0[0][1], 3)
+        for t in range(PACK):
+            s_gather(pairs0[1], 0, 0, t, S0[1][0], S0[1][1])
+            if t == 3:
+                order_copy(pairs1[0], pairs0[1], S0[1][1], 2)
 
-        v_grouped = []
-        for g in range(PASSES):
-            v_grouped.append(grouped_tile(g, 0, V_SLOTS))
-            nc.vector.tensor_copy(out=v_grouped[g][:], in_=picked[g][:].rearrange("p t n -> p n t"))
+        round_plane(1, 0)
+        v_grouped0 = join_pairs("v_grouped0", V0, pairs_v0[:], None)
+        round_plane(1, 1)
+        joined_a = join_pairs("joined0_a", S0[0][1], pairs0[0][:], "plane5")
+        quantize_x(0, 0, V0, v_grouped0[:])
+        round_plane(1, 2)
+        quantize_x(0, S0[0][0], S0[0][1], joined_a[:])
+        round_plane(1, 3)
+
+        pieces = len(PIECES)
+        for i, (first, n) in enumerate(PIECES):
+            for step, t in enumerate((3, 0, 1, 2)):
+                s_gather(pairs1[i], 0, 1, t, first, n)
+                if step == 1 and i + 1 < pieces:
+                    order_copy(pairs1[i + 1], pairs1[i], n, 3)
+
+        joined_b = join_pairs("joined0_b", S0[1][1], pairs0[1][:], "plane7")
         interleave_w(0)
-        quantize_x(0, 0, V_SLOTS, v_grouped[0][:])
+        quantize_x(0, S0[1][0], S0[1][1], joined_b[:])
         interleave_w(1)
-        quantize_x(1, 0, V_SLOTS, v_grouped[1][:])
         quantize_w(0)
-        multiply(0, V_SLOTS)
+        multiply(0, 0)
+        multiply(1, 0)
         interleave_w(2)
         quantize_w(1)
+        multiply(2, 0)
+        multiply(3, 0)
         interleave_w(3)
         quantize_w(2)
+        multiply(4, 0)
+        multiply(5, 0)
         quantize_w(3)
-        for i, (first, n) in enumerate(S_QUANT0):
-            lo = first - V_SLOTS
-            quantize_x(0, first, n, s_grouped0[:, lo : lo + n, :], after="w_grouped%d" % (2 + i))
+        multiply(6, 0)
+        multiply(7, 0)
 
-        done = [(0, V_SLOTS)] + list(S_PIECES)
-        hold = ["x_grouped0_%d" % V_SLOTS] + ["y%d" % first for first, n in done]
-        for i, (first, n) in enumerate(done):
-            finish(first, n)
-            if i + 1 < len(done):
-                nxt, m = done[i + 1]
-                quantize_x(1, nxt, m, s_grouped1[nxt][:], after=hold[i])
-                multiply(nxt, m)
-            scatter(first, n)
+        def experts_of(i):
+            first, n = PIECES[i]
+            return range(first // C, (first + n) // C)
+
+        def join_piece(i, after):
+            first, n = PIECES[i]
+            return join_pairs("joined1_%d" % i, n, pairs1[i][:], after)
+
+        def quantize_piece(i):
+            first, n = PIECES[i]
+            quantize_x(1, first, n, joined[i][:])
+            for e in experts_of(i):
+                multiply(e, 1)
+
+        hold = ["w_grouped2", "w_grouped3"] + [y_tag(i) for i in range(pieces)]
+        joined = {}
+        joined[0] = join_piece(0, hold[0])
+        joined[1] = join_piece(1, hold[1])
+        quantize_piece(0)
+        for i in range(pieces):
+            for e in experts_of(i):
+                finish(i, e)
+            if i + 1 < pieces:
+                quantize_piece(i + 1)
+            scatter(i)
+            if i + 2 < pieces:
+                joined[i + 2] = join_piece(i + 2, hold[i + 2])
 
         nc.sync.dma_start(out, window[:])

@@ -97,8 +97,8 @@ def tile_routed_moe_kernel(tc, xT, w, b, gate, offs, out):
         x_codes = {}
         x_scales = {}
 
-        def quantize_x(g, first, n, values):
-            codes = sb([P, n], U32, "x_codes%d_%d" % (g, first))
+        def quantize_x(g, first, n, values, after=None):
+            codes = sb([P, n], U32, "x_codes%d_%d" % (g, first), after)
             scales = sb([P, n], U8, "x_scales%d_%d" % (g, first))
             nc.vector.quantize_mx(out=codes[:].bitcast(FP8X4), scales=scales[:], in_=values.rearrange("p n t -> p (n t)"))
             for h in range(n // C):
@@ -111,7 +111,10 @@ def tile_routed_moe_kernel(tc, xT, w, b, gate, offs, out):
 
         def interleave_w(q):
             w_grouped[q] = sb([P, 4, N, PACK], BF16, "w_grouped%d" % q)
-            nc.vector.tensor_copy(out=w_grouped[q][:], in_=w_raw[q][:].rearrange("p a (j n) -> p a n j", j=PACK))
+            nc.vector.tensor_copy(
+                out=w_grouped[q][:].rearrange("p a (c i) j -> p a c j i", i=4),
+                in_=w_raw[q][:].rearrange("p a (j c i) -> p a c j i", j=PACK, i=4),
+            )
 
         def quantize_w(q):
             codes = sb([P, 4 * N], U32, "w_codes%d" % q)
@@ -172,17 +175,21 @@ def tile_routed_moe_kernel(tc, xT, w, b, gate, offs, out):
                 nc.vector.tensor_copy(window[:].indirect(list_of(lo, n)), sums[i][:])
 
         pairs_v0 = sb([P, 2, V0, 2], BF16, "pairs_v0")
-        pairs0 = [sb([P, 2, n, 2], BF16, "pairs0_%d" % first) for first, n in S0]
+        pairs0 = [sb([P, 2, S0[0][1], 2], BF16, "pairs0_a")]
+        joined_b = sb([P, S0[1][1], PACK], BF16, "joined0_b")
         pairs1 = [sb([P, 2, n, 2], BF16, "pairs1_%d" % first) for first, n in PIECES]
         for t in range(PACK):
             round_plane(0, t)
             nc.vector.tensor_copy(pairs_v0[:, t // 2, :, t % 2], planes[(0, t)][:].indirect(list_of(0, V0)))
             s_gather(pairs0[0], 0, 0, t, S0[0][0], S0[0][1])
-        order_copy(pairs0[1], pairs0[0], S0[0][1], 3)
+        nc.scalar.copy(out=joined_b[:, 0, :], in_=pairs0[0][:, 1, S0[0][1] - 4 : S0[0][1], 1])
         for t in range(PACK):
-            s_gather(pairs0[1], 0, 0, t, S0[1][0], S0[1][1])
+            nc.scalar.activation(joined_b[:, :, t], rounded(0, t).indirect(list_of(S0[1][0], S0[1][1])), COPY)
             if t == 3:
-                order_copy(pairs1[0], pairs0[1], S0[1][1], 2)
+                nc.scalar.copy(
+                    out=pairs1[0][:, :, 0, :],
+                    in_=joined_b[:, S0[1][1] - 4 : S0[1][1], 2].rearrange("p (a b) -> p a b", a=2),
+                )
 
         round_plane(1, 0)
         v_grouped0 = join_pairs("v_grouped0", V0, pairs_v0[:], None)
@@ -200,9 +207,8 @@ def tile_routed_moe_kernel(tc, xT, w, b, gate, offs, out):
                 if step == 1 and i + 1 < pieces:
                     order_copy(pairs1[i + 1], pairs1[i], n, 3)
 
-        joined_b = join_pairs("joined0_b", S0[1][1], pairs0[1][:], "plane7")
         interleave_w(0)
-        quantize_x(0, S0[1][0], S0[1][1], joined_b[:])
+        quantize_x(0, S0[1][0], S0[1][1], joined_b[:], "plane0")
         interleave_w(1)
         quantize_w(0)
         multiply(0, 0)

@@ -97,8 +97,8 @@ def tile_routed_moe_kernel(tc, xT, w, b, gate, offs, out):
         x_codes = {}
         x_scales = {}
 
-        def quantize_x(g, first, n, values, after=None):
-            codes = sb([P, n], U32, "x_codes%d_%d" % (g, first), after)
+        def quantize_x(g, first, n, values):
+            codes = sb([P, n], U32, "x_codes%d_%d" % (g, first))
             scales = sb([P, n], U8, "x_scales%d_%d" % (g, first))
             nc.vector.quantize_mx(out=codes[:].bitcast(FP8X4), scales=scales[:], in_=values.rearrange("p n t -> p (n t)"))
             for h in range(n // C):
@@ -175,21 +175,17 @@ def tile_routed_moe_kernel(tc, xT, w, b, gate, offs, out):
                 nc.vector.tensor_copy(window[:].indirect(list_of(lo, n)), sums[i][:])
 
         pairs_v0 = sb([P, 2, V0, 2], BF16, "pairs_v0")
-        pairs0 = [sb([P, 2, S0[0][1], 2], BF16, "pairs0_a")]
-        joined_b = sb([P, S0[1][1], PACK], BF16, "joined0_b")
+        pairs0 = [sb([P, 2, n, 2], BF16, "pairs0_%d" % first) for first, n in S0]
         pairs1 = [sb([P, 2, n, 2], BF16, "pairs1_%d" % first) for first, n in PIECES]
         for t in range(PACK):
             round_plane(0, t)
             nc.vector.tensor_copy(pairs_v0[:, t // 2, :, t % 2], planes[(0, t)][:].indirect(list_of(0, V0)))
             s_gather(pairs0[0], 0, 0, t, S0[0][0], S0[0][1])
-        nc.scalar.copy(out=joined_b[:, 0, :], in_=pairs0[0][:, 1, S0[0][1] - 4 : S0[0][1], 1])
+        order_copy(pairs0[1], pairs0[0], S0[0][1], 3)
         for t in range(PACK):
-            nc.scalar.activation(joined_b[:, :, t], rounded(0, t).indirect(list_of(S0[1][0], S0[1][1])), COPY)
+            s_gather(pairs0[1], 0, 0, t, S0[1][0], S0[1][1])
             if t == 3:
-                nc.scalar.copy(
-                    out=pairs1[0][:, :, 0, :],
-                    in_=joined_b[:, S0[1][1] - 4 : S0[1][1], 2].rearrange("p (a b) -> p a b", a=2),
-                )
+                order_copy(pairs1[0], pairs0[1], S0[1][1], 2)
 
         round_plane(1, 0)
         v_grouped0 = join_pairs("v_grouped0", V0, pairs_v0[:], None)
@@ -207,8 +203,9 @@ def tile_routed_moe_kernel(tc, xT, w, b, gate, offs, out):
                 if step == 1 and i + 1 < pieces:
                     order_copy(pairs1[i + 1], pairs1[i], n, 3)
 
+        joined_b = join_pairs("joined0_b", S0[1][1], pairs0[1][:], "plane7")
         interleave_w(0)
-        quantize_x(0, S0[1][0], S0[1][1], joined_b[:], "plane0")
+        quantize_x(0, S0[1][0], S0[1][1], joined_b[:])
         interleave_w(1)
         quantize_w(0)
         multiply(0, 0)

@@ -109,8 +109,8 @@ def tile_routed_moe_kernel(tc, xT, w, b, gate, offs, out):
         w_scales = {}
         w_grouped = {}
 
-        def interleave_w(q):
-            w_grouped[q] = sb([P, 4, N, PACK], BF16, "w_grouped%d" % q)
+        def interleave_w(q, after=None):
+            w_grouped[q] = sb([P, 4, N, PACK], BF16, "w_grouped%d" % q, after)
             nc.vector.tensor_copy(
                 out=w_grouped[q][:].rearrange("p a (c i) j -> p a c j i", i=4),
                 in_=w_raw[q][:].rearrange("p a (j c i) -> p a c j i", j=PACK, i=4),
@@ -214,13 +214,6 @@ def tile_routed_moe_kernel(tc, xT, w, b, gate, offs, out):
         quantize_w(1)
         multiply(2, 0)
         multiply(3, 0)
-        interleave_w(3)
-        quantize_w(2)
-        multiply(4, 0)
-        multiply(5, 0)
-        quantize_w(3)
-        multiply(6, 0)
-        multiply(7, 0)
 
         def experts_of(i):
             first, n = PIECES[i]
@@ -236,11 +229,18 @@ def tile_routed_moe_kernel(tc, xT, w, b, gate, offs, out):
             for e in experts_of(i):
                 multiply(e, 1)
 
-        hold = ["w_grouped2", "w_grouped3"] + [y_tag(i) for i in range(pieces)]
+        hold = ["w_grouped1", "pairs1_0"] + [y_tag(i) for i in range(pieces)]
         joined = {}
         joined[0] = join_piece(0, hold[0])
-        joined[1] = join_piece(1, hold[1])
+        interleave_w(3, "pairs1_0")
         quantize_piece(0)
+        quantize_w(2)
+        multiply(4, 0)
+        multiply(5, 0)
+        quantize_w(3)
+        multiply(6, 0)
+        multiply(7, 0)
+        joined[1] = join_piece(1, hold[1])
         for i in range(pieces):
             for e in experts_of(i):
                 finish(i, e)

@@ -112,8 +112,8 @@ def tile_routed_moe_kernel(tc, xT, w, b, gate, offs, out):
         def interleave_w(q, after=None):
             w_grouped[q] = sb([P, 4, N, PACK], BF16, "w_grouped%d" % q, after)
             nc.vector.tensor_copy(
-                out=w_grouped[q][:].rearrange("p a (c i) j -> p a c j i", i=4),
-                in_=w_raw[q][:].rearrange("p a (j c i) -> p a c j i", j=PACK, i=4),
+                out=w_grouped[q][:].rearrange("p a (c i) j -> p a c j i", i=8),
+                in_=w_raw[q][:].rearrange("p a (j c i) -> p a c j i", j=PACK, i=8),
             )
 
         def quantize_w(q):

from contextlib import ExitStack

import concourse.mybir as mybir

K, T, E, C, N = 1024, 2048, 8, 256, 128
FLOPS = 2 * K * E * C * N

F32 = mybir.dt.float32
BF16 = mybir.dt.bfloat16
U32 = mybir.dt.uint32
U16 = mybir.dt.uint16
U8 = mybir.dt.uint8
FP8X4 = mybir.dt.float8_e4m3fn_x4
MULT = mybir.AluOpType.mult
ADD = mybir.AluOpType.add
COPY = mybir.ActivationFunctionType.Copy
IDENTITY = mybir.ActivationFunctionType.Identity

P = 128
PACK = 4
PASSES = K // (P * PACK)
V0 = 512
S0 = ((512, 1024), (1536, 512))
PIECES = ((0, 512), (512, 512), (1024, 512), (1536, 512))
S_ROUNDS = ()
S_FINISH = (4, 5, 6, 7)


def tile_routed_moe_kernel(tc, xT, w, b, gate, offs, out):
    nc = tc.nc
    with ExitStack() as ctx:
        keep = ctx.enter_context(tc.tile_pool(name="keep", bufs=1))
        psum = ctx.enter_context(tc.psum_pool(name="psum", bufs=1))

        def sb(shape, dtype, name, tag=None):
            return keep.tile(shape, dtype, name=name, tag=(tag or name), align_bytes=64)

        offsets = keep.tile([P, E * C // 16], U16, name="offsets")
        nc.sync.dma_start(offsets[:], offs)
        b_sb = sb([P, E], F32, "b_sb")

        x_planes = xT.rearrange("(g p t) n -> g p t n", p=P, t=PACK)
        w_rows = w.rearrange("e (g p j) n -> p (e g) (j n)", g=PASSES, p=P, j=PACK)
        planes = {}
        for g in range(PASSES):
            for t in range(PACK):
                planes[(g, t)] = sb([P, T], F32, "plane%d" % (PACK * g + t))
                if (g, t) == (0, 0):
                    for h in range(2):
                        half = slice(h * T // 2, (h + 1) * T // 2)
                        nc.sync.dma_start(planes[(g, t)][:, half], x_planes[g, :, t, half])
                else:
                    nc.sync.dma_start(planes[(g, t)][:], x_planes[g, :, t, :])
        nc.sync.dma_start(b_sb[:], b)
        w_raw = {}
        for q in range(4):
            w_raw[q] = sb([P, 4, PACK * N], F32, "w_raw%d" % q, "plane%d" % q)
            nc.sync.dma_start(w_raw[q][:], w_rows[:, 4 * q : 4 * q + 4, :])
        gate_sb = sb([P, E * C], F32, "gate_sb", "plane4")
        nc.sync.dma_start(gate_sb[:], gate)
        window = sb([P, T], F32, "window", "plane6")

        halves = [sb([P, 2, T], BF16, "rounded%d" % i) for i in range(2 * PASSES)]

        def rounded(g, t):
            return halves[2 * g + t // 2][:, t % 2, :]

        def list_of(first, n):
            return offsets[:, first // 16 : (first + n) // 16]

        def round_plane(g, t):
            if (g, t) == (0, 0):
                for h in range(2):
                    half = slice(h * T // 2, (h + 1) * T // 2)
                    nc.vector.tensor_copy(out=rounded(g, t)[:, half], in_=planes[(g, t)][:, half])
            elif (g, t) in S_ROUNDS:
                nc.scalar.copy(out=rounded(g, t), in_=planes[(g, t)][:])
            else:
                nc.vector.tensor_copy(out=rounded(g, t), in_=planes[(g, t)][:])

        def s_gather(pairs, lo, g, t, first, n):
            nc.scalar.activation(pairs[:, t // 2, lo : lo + n, t % 2], rounded(g, t).indirect(list_of(first, n)), COPY)

        def order_copy(dst_pairs, src_pairs, n, t):
            nc.scalar.copy(
                out=dst_pairs[:, :, 0, :],
                in_=src_pairs[:, t // 2, n - 4 : n, t % 2].rearrange("p (a b) -> p a b", a=2),
            )

        def join_pairs(name, n, pairs, after):
            values = sb([P, n, PACK], BF16, name, after)
            nc.vector.tensor_copy(
                out=values[:].rearrange("p n (u e) -> p n u e", u=2), in_=pairs.rearrange("p u n e -> p n u e")
            )
            return values

        x_codes = {}
        x_scales = {}

        def quantize_x(g, first, n, values):
            codes = sb([P, n], U32, "x_codes%d_%d" % (g, first))
            scales = sb([P, n], U8, "x_scales%d_%d" % (g, first))
            nc.vector.quantize_mx(out=codes[:].bitcast(FP8X4), scales=scales[:], in_=values.rearrange("p n t -> p (n t)"))
            for h in range(n // C):
                x_codes[(first // C + h, g)] = codes[:, C * h : C * (h + 1)]
                x_scales[(first // C + h, g)] = scales[:, C * h : C * (h + 1)]

        w_codes = {}
        w_scales = {}
        w_grouped = {}

        def interleave_w(q, after=None):
            w_grouped[q] = sb([P, 4, N, PACK], BF16, "w_grouped%d" % q, after)
            nc.vector.tensor_copy(
                out=w_grouped[q][:].rearrange("p a (c i) j -> p a c j i", i=8),
                in_=w_raw[q][:].rearrange("p a (j c i) -> p a c j i", j=PACK, i=8),
            )

        def quantize_w(q):
            codes = sb([P, 4 * N], U32, "w_codes%d" % q)
            scales = sb([P, 4 * N], U8, "w_scales%d" % q)
            nc.vector.quantize_mx(
                out=codes[:].bitcast(FP8X4), scales=scales[:], in_=w_grouped[q][:].rearrange("p a n j -> p (a n j)")
            )
            for a in range(4):
                w_codes[(2 * q + a // 2, a % 2)] = codes[:, N * a : N * (a + 1)]
                w_scales[(2 * q + a // 2, a % 2)] = scales[:, N * a : N * (a + 1)]

        accs = {}

        def multiply(e, g):
            if g == 0:
                accs[e] = psum.tile([P, C], F32, name="acc%d" % e)
            nc.tensor.matmul_mx(
                out=accs[e][:],
                lhsT=w_codes[(e, g)].bitcast(FP8X4),
                lhsT_scale=w_scales[(e, g)],
                rhs=x_codes[(e, g)].bitcast(FP8X4),
                rhs_scale=x_scales[(e, g)],
                start=(g == 0),
                stop=(g == PASSES - 1),
            )

        sums = {}

        def y_tag(i):
            if i == 2:
                return "rounded3"
            if i == 3:
                return "rounded2"
            return "y%d" % i

        def finish(i, e):
            first, n = PIECES[i]
            if i not in sums:
                sums[i] = sb([P, n], F32, "y%d" % i, y_tag(i))
            y = sums[i][:, C * e - first : C * (e + 1) - first]
            if e in S_FINISH:
                nc.scalar.activation(out=y, in_=accs[e][:], func=IDENTITY, bias=b_sb[:, e : e + 1])
            else:
                nc.vector.scalar_tensor_tensor(
                    out=y,
                    in0=accs[e][:],
                    scalar=b_sb[:, e : e + 1],
                    in1=gate_sb[:, C * e : C * (e + 1)],
                    op0=ADD,
                    op1=MULT,
                )

        def scatter(i):
            lo, n = PIECES[i]
            if lo // C in S_FINISH:
                nc.vector.tensor_tensor(window[:].indirect(list_of(lo, n)), sums[i][:], gate_sb[:, lo : lo + n], MULT)
            else:
                nc.vector.tensor_copy(window[:].indirect(list_of(lo, n)), sums[i][:])

        pairs_v0 = sb([P, 2, V0, 2], BF16, "pairs_v0")
        pairs0 = [sb([P, 2, n, 2], BF16, "pairs0_%d" % first) for first, n in S0]
        pairs1 = [sb([P, 2, n, 2], BF16, "pairs1_%d" % first) for first, n in PIECES]
        for t in range(PACK):
            round_plane(0, t)
            nc.vector.tensor_copy(pairs_v0[:, t // 2, :, t % 2], planes[(0, t)][:].indirect(list_of(0, V0)))
            s_gather(pairs0[0], 0, 0, t, S0[0][0], S0[0][1])
        order_copy(pairs0[1], pairs0[0], S0[0][1], 3)
        for t in range(PACK):
            s_gather(pairs0[1], 0, 0, t, S0[1][0], S0[1][1])
            if t == 3:
                order_copy(pairs1[0], pairs0[1], S0[1][1], 2)

        round_plane(1, 0)
        v_grouped0 = join_pairs("v_grouped0", V0, pairs_v0[:], None)
        round_plane(1, 1)
        joined_a = join_pairs("joined0_a", S0[0][1], pairs0[0][:], "plane5")
        quantize_x(0, 0, V0, v_grouped0[:])
        round_plane(1, 2)
        quantize_x(0, S0[0][0], S0[0][1], joined_a[:])
        round_plane(1, 3)

        pieces = len(PIECES)
        for i, (first, n) in enumerate(PIECES):
            for step, t in enumerate((3, 0, 1, 2)):
                s_gather(pairs1[i], 0, 1, t, first, n)
                if step == 1 and i + 1 < pieces:
                    order_copy(pairs1[i + 1], pairs1[i], n, 3)

        joined_b = join_pairs("joined0_b", S0[1][1], pairs0[1][:], "plane7")
        interleave_w(0)
        quantize_x(0, S0[1][0], S0[1][1], joined_b[:])
        interleave_w(1)
        quantize_w(0)
        multiply(0, 0)
        multiply(1, 0)
        interleave_w(2)
        quantize_w(1)
        multiply(2, 0)
        multiply(3, 0)

        def experts_of(i):
            first, n = PIECES[i]
            return range(first // C, (first + n) // C)

        def join_piece(i, after):
            first, n = PIECES[i]
            return join_pairs("joined1_%d" % i, n, pairs1[i][:], after)

        def quantize_piece(i):
            first, n = PIECES[i]
            quantize_x(1, first, n, joined[i][:])
            for e in experts_of(i):
                multiply(e, 1)

        hold = ["w_grouped1", "pairs1_0"] + [y_tag(i) for i in range(pieces)]
        joined = {}
        joined[0] = join_piece(0, hold[0])
        interleave_w(3, "pairs1_0")
        quantize_piece(0)
        quantize_w(2)
        multiply(4, 0)
        multiply(5, 0)
        quantize_w(3)
        multiply(6, 0)
        multiply(7, 0)
        joined[1] = join_piece(1, hold[1])
        for i in range(pieces):
            for e in experts_of(i):
                finish(i, e)
            if i + 1 < pieces:
                quantize_piece(i + 1)
            scatter(i)
            if i + 2 < pieces:
                joined[i + 2] = join_piece(i + 2, hold[i + 2])

        nc.sync.dma_start(out, window[:])
